import numpy as np
import ml_dtypes


def mxq(x, axis, fmt="e4m3"):
    dtype, down = {"e4m3": (ml_dtypes.float8_e4m3fn, 7), "e5m2": (ml_dtypes.float8_e5m2, 14)}[fmt]
    v = np.moveaxis(np.asarray(x, np.float32).astype(ml_dtypes.bfloat16).astype(np.float64), axis, -1)
    blocks = v.reshape(v.shape[:-1] + (-1, 32))
    amax = np.abs(blocks).max(-1, keepdims=True)
    byte = np.maximum(np.where(amax > 0, np.frexp(amax)[1] - 1 + 127, 0) - down, 1)
    scale = np.exp2(byte - 127.0)
    codes = (blocks / scale).astype(np.float32).astype(dtype).astype(np.float64)
    return np.moveaxis((codes * scale).reshape(v.shape), -1, axis)


WIDE = False


def mx_kscale(k):
    if not WIDE:
        return np.ones(k)
    levels = np.array([10, -10, 5, -5, 0])
    if k % 512:
        return np.exp2(np.random.permutation(np.resize(levels, k // 32))).repeat(32)
    a = np.empty((k // 512, 16))
    for p in range(k // 512):
        a[p, :8] = np.random.permutation(np.resize(levels, 8))
        for g in range(8):
            far = levels[np.abs(levels - a[p, g]) >= 10]
            a[p, g + 8] = far[np.random.randint(len(far))]
    return np.exp2(a.ravel()).repeat(32)


def f64(x):
    return np.asarray(x).astype(np.float64)


def striped8(idx):
    return np.concatenate([x.reshape(-1, 16).T for x in idx]).astype(np.uint16)


def runs(offs, k):
    lists = np.stack([offs[16 * r : 16 * r + 16].T.reshape(-1) for r in range(8)]).astype(np.int64)
    return lists[np.arange(k) % 512 // 64]


def pack_weight(w):
    k, n = w.shape
    w = f64(np.asarray(w, np.float32).astype(ml_dtypes.bfloat16)).reshape(k // 32, 32, n)
    amax = np.abs(w).max(1)
    byte = np.clip(np.where(amax > 0, np.frexp(amax)[1] - 1 + 127 - 7, 1), 1, 254)
    scaled = (w * np.exp2(127.0 - byte)[:, None, :]).reshape(k, n).astype(np.float32)
    words = np.ascontiguousarray(scaled.reshape(k // 512, 128, 4, n).transpose(0, 1, 3, 2)).astype(ml_dtypes.float8_e4m3fn).view(np.uint8)
    return words, np.ascontiguousarray(byte.astype(np.uint8).reshape(k // 512, 16, n))


def unpack_weight(words, scales):
    g, p, n, _ = words.shape
    vals = np.ascontiguousarray(words).view(ml_dtypes.float8_e4m3fn).astype(np.float64) * np.repeat(np.exp2(scales.astype(np.float64) - 127.0), 8, axis=1)[..., None]
    return vals.transpose(0, 1, 3, 2).reshape(g * 512, n)


def relu(v):
    return np.maximum(v, 0.0)


K, T, S, N, H = 512, 2048, 512, 512, 512


def setup_inputs():
    n = np.random.standard_normal
    s = mx_kscale(K)[:, None]
    u = mx_kscale(H)
    packed_xT = pack_weight(n((K, T)) * s)
    return {
        "x_words": packed_xT[0],
        "x_scales": packed_xT[1],
        "w1": (n((K, H)) / np.sqrt(K) / s).astype(np.float32),
        "gn": (np.random.uniform(0.5, 1.5, (H, 1)) * u[:, None]).astype(np.float32),
        "w2": (n((H, N)) / np.sqrt(H) / u[:, None]).astype(np.float32),
        "offs": striped8(np.random.randint(0, T, (8, S))),
        "n1": striped8(np.stack([np.random.permutation(S) for _ in range(8)])),
        "n2": striped8(np.stack([np.random.permutation(S) for _ in range(8)])),
        "n3": striped8(np.stack([np.random.permutation(S) for _ in range(8)])),
        "n4": striped8(np.stack([np.random.permutation(S) for _ in range(8)])),
    }


def reference(x_words, x_scales, w1, gn, w2, offs, n1, n2, n3, n4):
    xq = unpack_weight(x_words, x_scales)[np.arange(K)[:, None], runs(offs, K)]
    y = mxq(f64(w1), 0, "e4m3").T @ xq
    z = f64(gn) * (relu(y - (y[np.arange(H)[:, None], runs(n1, H)])) + 0.5 * (relu(y[np.arange(H)[:, None], runs(n2, H)] - y)))
    h = mxq(f64(w2), 0, "e4m3").T @ mxq(z, 0, "e4m3")
    return (h - (h[np.arange(N)[:, None], runs(n3, N)])) / (np.abs(h[np.arange(N)[:, None], runs(n4, N)] - h) + 0.5)

@@ -1,0 +1,221 @@
+from contextlib import ExitStack
+
+import concourse.mybir as mybir
+
+K, T, S, H, N = 512, 2048, 512, 512, 512
+FLOPS = 2 * K * H * S + 2 * H * N * S
+
+F32 = mybir.dt.float32
+BF16 = mybir.dt.bfloat16
+I32 = mybir.dt.int32
+U32 = mybir.dt.uint32
+U16 = mybir.dt.uint16
+U8 = mybir.dt.uint8
+FP8X4 = mybir.dt.float8_e4m3fn_x4
+ALU = mybir.AluOpType
+ACT = mybir.ActivationFunctionType
+
+P = 128
+PACK = 4
+HALF = S // 2
+
+
+def entries(lists, first, count):
+    return lists[:, first // 16 : (first + count) // 16]
+
+
+def tile_picked_hashhingefrac_none_p_kernel(
+    tc, x_words, x_scales, w1, gn, w2, offs, n1, n2, n3, n4, out
+):
+    nc = tc.nc
+    with ExitStack() as ctx:
+        held = ctx.enter_context(tc.tile_pool(name="held", bufs=1))
+        psum = ctx.enter_context(tc.psum_pool(name="psum", bufs=8))
+
+        offs_sb = held.tile([P, S // 16], U16, name="offs_sb")
+        nc.sync.dma_start(offs_sb[:], offs)
+
+        scale_table = held.tile([P, T], U8, name="scale_table", tag="scales_then_w2", align_bytes=64)
+        nc.vector.memset(scale_table[:].bitcast(I32), 0)
+        nc.scalar.dma_start(scale_table[0:P:8, :].bitcast(I32), x_scales[0].bitcast(I32))
+        x_plane = held.tile([P, S], U8, name="x_plane", align_bytes=64)
+        nc.vector.memset(x_plane[:].bitcast(I32), 0)
+
+        w1_raw = held.tile([P, PACK, H], F32, name="w1_raw")
+        nc.sync.dma_start(w1_raw[:], w1.rearrange("(p j) c -> p j c", j=PACK))
+        gain = held.tile([P, PACK], F32, name="gain")
+        nc.sync.dma_start(gain[:], gn.rearrange("(p t) o -> p (t o)", t=PACK))
+        lists = []
+        for name, src in (("n2_sb", n2), ("n1_sb", n1), ("n4_sb", n4), ("n3_sb", n3)):
+            lst = held.tile([P, S // 16], U16, name=name)
+            nc.sync.dma_start(lst[:], src)
+            lists.append(lst)
+        n2_sb, n1_sb, n4_sb, n3_sb = lists
+        word_table = held.tile([P, T], U32, name="word_table", align_bytes=64)
+        nc.sync.dma_start(word_table[:].bitcast(I32), x_words[0].rearrange("p n t -> p (n t)").bitcast(I32))
+
+        warm_in = held.tile([P, 1], F32, name="warm_in")
+        warm_out = held.tile([P, 1], F32, name="warm_out")
+        nc.vector.memset(warm_in[:], 1.0)
+        nc.scalar.activation(warm_out[:], warm_in[:], ACT.Abs_reciprocal_sqrt)
+
+        picked_scales = held.tile([P, S], U8, name="picked_scales", align_bytes=64)
+        nc.vector.tensor_copy(picked_scales[:], scale_table[:].indirect(offs_sb[:]))
+        for q in range(4):
+            nc.scalar.dma_start(
+                x_plane[32 * q : 32 * q + 4, :].bitcast(I32),
+                picked_scales[32 * q : 32 * q + 32 : 8, :].bitcast(I32),
+            )
+
+        w2_raw = held.tile([P, PACK, N], F32, name="w2_raw", tag="scales_then_w2", align_bytes=64)
+        nc.sync.dma_start(w2_raw[:], w2.rearrange("(p j) c -> p j c", j=PACK))
+
+        w1_bf = held.tile([P, PACK * H], BF16, name="w1_bf", align_bytes=64)
+        nc.vector.tensor_copy(
+            w1_bf[:].rearrange("p (t m j) -> p m j t", t=PACK, j=PACK),
+            w1_raw[:].rearrange("p j (m t) -> p m j t", t=PACK),
+        )
+        w1_codes = held.tile([P, H], U32, name="w1_codes", align_bytes=64)
+        w1_plane = held.tile([P, H], U8, name="w1_plane", align_bytes=64)
+        nc.vector.quantize_mx(w1_codes[:].bitcast(FP8X4), w1_plane[:], w1_bf[:])
+
+        gain_abs = held.tile([P, PACK], F32, name="gain_abs")
+        nc.scalar.activation(gain_abs[:], gain[:], ACT.Abs)
+        negative = held.tile([P, PACK], F32, name="negative")
+        flip = held.tile([P, PACK], F32, name="flip")
+        nc.vector.tensor_scalar(negative[:], gain[:], 0.0, 2.0, ALU.is_lt, ALU.mult)
+        nc.vector.tensor_scalar_add(flip[:], negative[:], -1.0)
+
+        y_window = [held.tile([P, S], F32, name="y_window%d" % t) for t in range(PACK)]
+        y_plain = [held.tile([P, S], F32, name="y_plain%d" % t) for t in range(PACK)]
+        y_banks = {}
+        for half in range(2):
+            cols = slice(half * HALF, (half + 1) * HALF)
+            x_codes = held.tile([P, HALF], U32, name="x_codes%d" % half, align_bytes=64)
+            nc.vector.tensor_copy(x_codes[:], word_table[:].indirect(entries(offs_sb, half * HALF, HALF)))
+            for t in range(PACK):
+                bank = psum.tile([P, S], F32, name="bank")
+                rows = slice(t * P, (t + 1) * P)
+                nc.tensor.matmul_mx(
+                    bank[:, :HALF],
+                    lhsT=w1_codes[:, rows].bitcast(FP8X4),
+                    lhsT_scale=w1_plane[:, rows],
+                    rhs=x_codes[:].bitcast(FP8X4),
+                    rhs_scale=x_plane[:, cols],
+                    start=True,
+                    stop=True,
+                )
+                y_banks[half, t] = bank
+        for t in range(PACK):
+            for target, half in ((y_window, 0), (y_plain, 0), (y_window, 1)):
+                cols = slice(half * HALF, (half + 1) * HALF)
+                nc.scalar.activation(target[t][:, cols], y_banks[half, t][:, :HALF], ACT.Copy, scale=gain_abs[:, t : t + 1])
+        for t in range(PACK):
+            nc.scalar.activation(y_plain[t][:, HALF:], y_banks[1, t][:, :HALF], ACT.Copy, scale=gain_abs[:, t : t + 1])
+
+        w2_signed = held.tile([P, PACK, N], BF16, name="w2_signed")
+        w2_bf = held.tile([P, PACK * N], BF16, name="w2_bf", align_bytes=64)
+        w2_codes = held.tile([P, N], U32, name="w2_codes", align_bytes=64)
+        w2_plane = held.tile([P, N], U8, name="w2_plane", align_bytes=64)
+        h_window = [held.tile([P, S], F32, name="h_window%d" % t) for t in range(PACK)]
+        h_plain = [held.tile([P, S], F32, name="h_plain%d" % t) for t in range(PACK)]
+
+        def gather_y(target, t, lst, half):
+            nc.vector.tensor_tensor(
+                target[:, t, :],
+                y_window[t][:].indirect(entries(lst, half * HALF, HALF)),
+                y_plain[t][:, half * HALF : (half + 1) * HALF],
+                ALU.subtract,
+            )
+
+        def half_relu(up, half):
+            up_relu = held.tile([P, HALF, PACK], F32, name="up_relu%d" % half)
+            nc.scalar.activation(up_relu[:], up[:].rearrange("p t j -> p j t"), ACT.Relu, scale=0.5)
+            return up_relu
+
+        def second_product(half, down, up_relu):
+            z_bf = held.tile([P, HALF, PACK], BF16, name="z_bf%d" % half, align_bytes=64)
+            nc.vector.scalar_tensor_tensor(
+                z_bf[:], down[:].rearrange("p t j -> p j t"), 0.0, up_relu[:], ALU.min, ALU.subtract
+            )
+            z_codes = held.tile([P, HALF], U32, name="z_codes%d" % half, align_bytes=64)
+            z_plane = held.tile([P, HALF], U8, name="z_plane%d" % half, align_bytes=64)
+            nc.vector.quantize_mx(z_codes[:].bitcast(FP8X4), z_plane[:], z_bf[:].rearrange("p j t -> p (j t)"))
+            banks = []
+            for t in range(PACK):
+                bank = psum.tile([P, S], F32, name="bank")
+                rows = slice(t * P, (t + 1) * P)
+                nc.tensor.matmul_mx(
+                    bank[:, :HALF],
+                    lhsT=w2_codes[:, rows].bitcast(FP8X4),
+                    lhsT_scale=w2_plane[:, rows],
+                    rhs=z_codes[:].bitcast(FP8X4),
+                    rhs_scale=z_plane[:],
+                    start=True,
+                    stop=True,
+                )
+                banks.append(bank)
+            for t in range(PACK):
+                for target in (h_window, h_plain):
+                    nc.scalar.copy(target[t][:, half * HALF : (half + 1) * HALF], banks[t][:, :HALF])
+
+        up0 = held.tile([P, PACK, HALF], F32, name="up0")
+        down0 = held.tile([P, PACK, HALF], F32, name="down", tag="down")
+        for t in range(PACK):
+            gather_y(up0, t, n2_sb, 0)
+            gather_y(down0, t, n1_sb, 0)
+        for j in range(PACK):
+            nc.scalar.activation(w2_signed[:, j, :], w2_raw[:, j, :], ACT.Copy, scale=flip[:, j : j + 1])
+        up_relu0 = half_relu(up0, 0)
+        up1 = held.tile([P, PACK, HALF], F32, name="up1")
+        for t in range(PACK):
+            gather_y(up1, t, n2_sb, 1)
+        up_relu1 = half_relu(up1, 1)
+        nc.vector.tensor_copy(
+            w2_bf[:].rearrange("p (t m j) -> p m j t", t=PACK, j=PACK),
+            w2_signed[:].rearrange("p j (m t) -> p m j t", t=PACK),
+        )
+        nc.vector.quantize_mx(w2_codes[:].bitcast(FP8X4), w2_plane[:], w2_bf[:])
+        second_product(0, down0, up_relu0)
+        down1 = held.tile([P, PACK, HALF], F32, name="down", tag="down")
+        for t in range(PACK):
+            gather_y(down1, t, n1_sb, 1)
+        second_product(1, down1, up_relu1)
+
+        out_rows = out.rearrange("(p t) j -> p t j", t=PACK)
+
+        def gathered_difference(name, t, lst, halves):
+            diff = held.tile([P, S], F32, name=name)
+            for half in halves:
+                cols = slice(half * HALF, (half + 1) * HALF)
+                nc.vector.tensor_tensor(
+                    diff[:, cols],
+                    h_window[t][:].indirect(entries(lst, half * HALF, HALF)),
+                    h_plain[t][:, cols],
+                    ALU.subtract,
+                )
+            return diff
+
+        def denominator(t):
+            diff = gathered_difference("den%d" % t, t, n4_sb, range(2))
+            size = held.tile([P, S], F32, name="size%d" % t)
+            root = held.tile([P, S], F32, name="root%d" % t)
+            recip = held.tile([P, S], F32, name="recip%d" % t)
+            nc.scalar.activation(size[:], diff[:], ACT.Abs)
+            nc.scalar.activation(root[:], size[:], ACT.Abs_reciprocal_sqrt, bias=0.5)
+            nc.scalar.activation(recip[:], root[:], ACT.Square)
+            return recip
+
+        def quotient(t, recip):
+            diff = gathered_difference("num%d" % t, t, n3_sb, range(2))
+            result = held.tile([P, S], F32, name="result%d" % t)
+            for half in range(2):
+                cols = slice(half * HALF, (half + 1) * HALF)
+                nc.vector.scalar_tensor_tensor(result[:, cols], diff[:, cols], -1.0, recip[:, cols], ALU.mult, ALU.mult)
+                nc.sync.dma_start(out_rows[:, t, cols], result[:, cols])
+
+        recip = denominator(0)
+        for t in range(PACK):
+            following = denominator(t + 1) if t + 1 < PACK else None
+            quotient(t, recip)
+            recip = following

@@ -24,6 +24,10 @@ def entries(lists, first, count):
     return lists[:, first // 16 : (first + count) // 16]
 
 
+def half_cols(half):
+    return slice(half * HALF, (half + 1) * HALF)
+
+
 def tile_picked_hashhingefrac_none_p_kernel(
     tc, x_words, x_scales, w1, gn, w2, offs, n1, n2, n3, n4, out
 ):
@@ -35,14 +39,12 @@ def tile_picked_hashhingefrac_none_p_kernel(
         offs_sb = held.tile([P, S // 16], U16, name="offs_sb")
         nc.sync.dma_start(offs_sb[:], offs)
 
-        scale_table = held.tile([P, T], U8, name="scale_table", tag="scales_then_w2", align_bytes=64)
-        nc.vector.memset(scale_table[:].bitcast(I32), 0)
+        scale_table = held.tile([P, T], U8, name="scale_table", tag="scales_then_w1", align_bytes=64)
+        nc.gpsimd.memset(scale_table[:].bitcast(I32), 0)
         nc.scalar.dma_start(scale_table[0:P:8, :].bitcast(I32), x_scales[0].bitcast(I32))
         x_plane = held.tile([P, S], U8, name="x_plane", align_bytes=64)
-        nc.vector.memset(x_plane[:].bitcast(I32), 0)
+        nc.gpsimd.memset(x_plane[:].bitcast(I32), 0)
 
-        w1_raw = held.tile([P, PACK, H], F32, name="w1_raw")
-        nc.sync.dma_start(w1_raw[:], w1.rearrange("(p j) c -> p j c", j=PACK))
         gain = held.tile([P, PACK], F32, name="gain")
         nc.sync.dma_start(gain[:], gn.rearrange("(p t) o -> p (t o)", t=PACK))
         lists = []
@@ -51,171 +53,162 @@ def tile_picked_hashhingefrac_none_p_kernel(
             nc.sync.dma_start(lst[:], src)
             lists.append(lst)
         n2_sb, n1_sb, n4_sb, n3_sb = lists
+        w1_raw = held.tile([P, PACK, H], F32, name="w1_raw")
+        nc.sync.dma_start(w1_raw[:], w1.rearrange("(p j) c -> p j c", j=PACK))
         word_table = held.tile([P, T], U32, name="word_table", align_bytes=64)
         nc.sync.dma_start(word_table[:].bitcast(I32), x_words[0].rearrange("p n t -> p (n t)").bitcast(I32))
+
+        window = [held.tile([P, 2 * S], F32, name="window%d" % t) for t in range(PACK)]
+        for t in range(PACK):
+            nc.gpsimd.memset(window[t][:, S:], 0.0)
 
         warm_in = held.tile([P, 1], F32, name="warm_in")
         warm_out = held.tile([P, 1], F32, name="warm_out")
         nc.vector.memset(warm_in[:], 1.0)
         nc.scalar.activation(warm_out[:], warm_in[:], ACT.Abs_reciprocal_sqrt)
 
-        picked_scales = held.tile([P, S], U8, name="picked_scales", align_bytes=64)
+        picked_scales = held.tile([P, S], U8, name="picked_scales", tag="picked_then_w2", align_bytes=64)
         nc.vector.tensor_copy(picked_scales[:], scale_table[:].indirect(offs_sb[:]))
         for q in range(4):
             nc.scalar.dma_start(
                 x_plane[32 * q : 32 * q + 4, :].bitcast(I32),
                 picked_scales[32 * q : 32 * q + 32 : 8, :].bitcast(I32),
             )
-
-        w2_raw = held.tile([P, PACK, N], F32, name="w2_raw", tag="scales_then_w2", align_bytes=64)
+        w2_raw = held.tile([P, PACK, N], F32, name="w2_raw", tag="picked_then_w2", align_bytes=64)
         nc.sync.dma_start(w2_raw[:], w2.rearrange("(p j) c -> p j c", j=PACK))
 
-        w1_bf = held.tile([P, PACK * H], BF16, name="w1_bf", align_bytes=64)
-        nc.vector.tensor_copy(
-            w1_bf[:].rearrange("p (t m j) -> p m j t", t=PACK, j=PACK),
-            w1_raw[:].rearrange("p j (m t) -> p m j t", t=PACK),
-        )
         w1_codes = held.tile([P, H], U32, name="w1_codes", align_bytes=64)
         w1_plane = held.tile([P, H], U8, name="w1_plane", align_bytes=64)
-        nc.vector.quantize_mx(w1_codes[:].bitcast(FP8X4), w1_plane[:], w1_bf[:])
+        w1_dealt = w1_raw[:].rearrange("p j (m t) -> p m j t", t=PACK)
+        w1_low = held.tile([P, 2 * H], BF16, name="w1_low", tag="scales_then_w1", align_bytes=64)
+        w1_high = held.tile([P, 2 * H], BF16, name="w1_high", align_bytes=64)
+        nc.vector.tensor_copy(w1_low[:].rearrange("p (t m j) -> p m j t", t=2, j=PACK), w1_dealt[:, :, :, 0:2])
+        nc.scalar.copy(w1_high[:].rearrange("p (t m j) -> p m j t", t=2, j=PACK), w1_dealt[:, :, :, 2:4])
+        for pair, w1_bf in enumerate((w1_low, w1_high)):
+            cols = slice(pair * 2 * P, (pair + 1) * 2 * P)
+            nc.vector.quantize_mx(w1_codes[:, cols].bitcast(FP8X4), w1_plane[:, cols], w1_bf[:])
 
         gain_abs = held.tile([P, PACK], F32, name="gain_abs")
         nc.scalar.activation(gain_abs[:], gain[:], ACT.Abs)
         negative = held.tile([P, PACK], F32, name="negative")
-        flip = held.tile([P, PACK], F32, name="flip")
-        nc.vector.tensor_scalar(negative[:], gain[:], 0.0, 2.0, ALU.is_lt, ALU.mult)
-        nc.vector.tensor_scalar_add(flip[:], negative[:], -1.0)
+        gain_sign = held.tile([P, PACK], F32, name="gain_sign")
+        nc.vector.tensor_scalar(negative[:], gain[:], 0.0, -2.0, ALU.is_lt, ALU.mult)
+        nc.vector.tensor_scalar_add(gain_sign[:], negative[:], 1.0)
 
-        y_window = [held.tile([P, S], F32, name="y_window%d" % t) for t in range(PACK)]
+        def product(w_codes, w_plane, codes, plane, t, first, count):
+            bank = psum.tile([P, S], F32, name="bank")
+            rows = slice(t * P, (t + 1) * P)
+            cols = slice(first, first + count)
+            nc.tensor.matmul_mx(
+                bank[:, :count],
+                lhsT=w_codes[:, rows].bitcast(FP8X4),
+                lhsT_scale=w_plane[:, rows],
+                rhs=codes[:, cols].bitcast(FP8X4),
+                rhs_scale=plane[:, cols],
+                start=True,
+                stop=True,
+            )
+            return bank[:, :count]
+
+        def gather_difference(target, t, lst, plain, first, count):
+            cols = slice(first, first + count)
+            nc.vector.tensor_tensor(
+                target[:, cols], window[t][:].indirect(entries(lst, first, count)), plain[:, cols], ALU.subtract
+            )
+
+        halves = ((0, HALF), (HALF, HALF))
+        whole = ((0, S),)
+        x_codes = held.tile([P, S], U32, name="x_codes", align_bytes=64)
+        for first, count in halves:
+            nc.vector.tensor_copy(x_codes[:, first : first + count], word_table[:].indirect(entries(offs_sb, first, count)))
         y_plain = [held.tile([P, S], F32, name="y_plain%d" % t) for t in range(PACK)]
-        y_banks = {}
-        for half in range(2):
-            cols = slice(half * HALF, (half + 1) * HALF)
-            x_codes = held.tile([P, HALF], U32, name="x_codes%d" % half, align_bytes=64)
-            nc.vector.tensor_copy(x_codes[:], word_table[:].indirect(entries(offs_sb, half * HALF, HALF)))
-            for t in range(PACK):
-                bank = psum.tile([P, S], F32, name="bank")
-                rows = slice(t * P, (t + 1) * P)
-                nc.tensor.matmul_mx(
-                    bank[:, :HALF],
-                    lhsT=w1_codes[:, rows].bitcast(FP8X4),
-                    lhsT_scale=w1_plane[:, rows],
-                    rhs=x_codes[:].bitcast(FP8X4),
-                    rhs_scale=x_plane[:, cols],
-                    start=True,
-                    stop=True,
-                )
-                y_banks[half, t] = bank
         for t in range(PACK):
-            for target, half in ((y_window, 0), (y_plain, 0), (y_window, 1)):
-                cols = slice(half * HALF, (half + 1) * HALF)
-                nc.scalar.activation(target[t][:, cols], y_banks[half, t][:, :HALF], ACT.Copy, scale=gain_abs[:, t : t + 1])
-        for t in range(PACK):
-            nc.scalar.activation(y_plain[t][:, HALF:], y_banks[1, t][:, :HALF], ACT.Copy, scale=gain_abs[:, t : t + 1])
+            for first, count in halves if t == 0 else whole:
+                cols = slice(first, first + count)
+                bank = product(w1_codes, w1_plane, x_codes, x_plane, t, first, count)
+                nc.scalar.activation(window[t][:, cols], bank, ACT.Copy, scale=gain_abs[:, t : t + 1])
+                if t < 2:
+                    nc.scalar.activation(y_plain[t][:, cols], bank, ACT.Copy, scale=gain_abs[:, t : t + 1])
+            if t >= 2:
+                nc.sync.dma_start(y_plain[t][:], window[t][:, :S])
 
         w2_signed = held.tile([P, PACK, N], BF16, name="w2_signed")
-        w2_bf = held.tile([P, PACK * N], BF16, name="w2_bf", align_bytes=64)
+        w2_bf = held.tile([P, N, PACK], BF16, name="w2_bf", align_bytes=64)
         w2_codes = held.tile([P, N], U32, name="w2_codes", align_bytes=64)
         w2_plane = held.tile([P, N], U8, name="w2_plane", align_bytes=64)
-        h_window = [held.tile([P, S], F32, name="h_window%d" % t) for t in range(PACK)]
-        h_plain = [held.tile([P, S], F32, name="h_plain%d" % t) for t in range(PACK)]
-
-        def gather_y(target, t, lst, half):
-            nc.vector.tensor_tensor(
-                target[:, t, :],
-                y_window[t][:].indirect(entries(lst, half * HALF, HALF)),
-                y_plain[t][:, half * HALF : (half + 1) * HALF],
-                ALU.subtract,
+        for j in range(PACK):
+            nc.scalar.activation(
+                w2_signed[:, j, :].rearrange("p (t m) -> p m t", t=PACK),
+                w2_raw[:, j, :].rearrange("p (m t) -> p m t", t=PACK),
+                ACT.Copy,
+                scale=gain_sign[:, j : j + 1],
             )
+        nc.scalar.copy(
+            w2_bf[:].rearrange("p (c i) j -> p c j i", i=4),
+            w2_signed[:].rearrange("p j (c i) -> p c j i", i=4),
+        )
 
-        def half_relu(up, half):
+        up = held.tile([P, PACK, S], F32, name="up")
+        down = held.tile([P, PACK, S], F32, name="down")
+        for first, count in halves:
+            gather_difference(up[:, 0, :], 0, n2_sb, y_plain[0], first, count)
+            gather_difference(down[:, 0, :], 0, n1_sb, y_plain[0], first, count)
+        gather_difference(up[:, 1, :], 1, n2_sb, y_plain[1], 0, S)
+        gather_difference(down[:, 1, :], 1, n1_sb, y_plain[1], 0, S)
+        for target, lst in ((up, n2_sb), (down, n1_sb)):
+            for t in range(2, PACK):
+                gather_difference(target[:, t, :], t, lst, y_plain[t], 0, S)
+        nc.vector.quantize_mx(w2_codes[:].bitcast(FP8X4), w2_plane[:], w2_bf[:].rearrange("p c j -> p (c j)"))
+
+        z_codes = held.tile([P, S], U32, name="z_codes", align_bytes=64)
+        z_plane = held.tile([P, S], U8, name="z_plane", align_bytes=64)
+        for half in range(2):
+            cols = half_cols(half)
             up_relu = held.tile([P, HALF, PACK], F32, name="up_relu%d" % half)
-            nc.scalar.activation(up_relu[:], up[:].rearrange("p t j -> p j t"), ACT.Relu, scale=0.5)
-            return up_relu
-
-        def second_product(half, down, up_relu):
+            nc.scalar.activation(up_relu[:], up[:, :, cols].rearrange("p t j -> p j t"), ACT.Relu, scale=0.5)
             z_bf = held.tile([P, HALF, PACK], BF16, name="z_bf%d" % half, align_bytes=64)
             nc.vector.scalar_tensor_tensor(
-                z_bf[:], down[:].rearrange("p t j -> p j t"), 0.0, up_relu[:], ALU.min, ALU.subtract
+                z_bf[:], down[:, :, cols].rearrange("p t j -> p j t"), 0.0, up_relu[:], ALU.min, ALU.subtract
             )
-            z_codes = held.tile([P, HALF], U32, name="z_codes%d" % half, align_bytes=64)
-            z_plane = held.tile([P, HALF], U8, name="z_plane%d" % half, align_bytes=64)
-            nc.vector.quantize_mx(z_codes[:].bitcast(FP8X4), z_plane[:], z_bf[:].rearrange("p j t -> p (j t)"))
-            banks = []
-            for t in range(PACK):
-                bank = psum.tile([P, S], F32, name="bank")
-                rows = slice(t * P, (t + 1) * P)
-                nc.tensor.matmul_mx(
-                    bank[:, :HALF],
-                    lhsT=w2_codes[:, rows].bitcast(FP8X4),
-                    lhsT_scale=w2_plane[:, rows],
-                    rhs=z_codes[:].bitcast(FP8X4),
-                    rhs_scale=z_plane[:],
-                    start=True,
-                    stop=True,
-                )
-                banks.append(bank)
-            for t in range(PACK):
-                for target in (h_window, h_plain):
-                    nc.scalar.copy(target[t][:, half * HALF : (half + 1) * HALF], banks[t][:, :HALF])
+            nc.vector.quantize_mx(
+                z_codes[:, cols].bitcast(FP8X4), z_plane[:, cols], z_bf[:].rearrange("p j t -> p (j t)")
+            )
 
-        up0 = held.tile([P, PACK, HALF], F32, name="up0")
-        down0 = held.tile([P, PACK, HALF], F32, name="down", tag="down")
+        h_plain = [held.tile([P, S], F32, name="h_plain%d" % t) for t in range(PACK)]
         for t in range(PACK):
-            gather_y(up0, t, n2_sb, 0)
-            gather_y(down0, t, n1_sb, 0)
-        for j in range(PACK):
-            nc.scalar.activation(w2_signed[:, j, :], w2_raw[:, j, :], ACT.Copy, scale=flip[:, j : j + 1])
-        up_relu0 = half_relu(up0, 0)
-        up1 = held.tile([P, PACK, HALF], F32, name="up1")
-        for t in range(PACK):
-            gather_y(up1, t, n2_sb, 1)
-        up_relu1 = half_relu(up1, 1)
-        nc.vector.tensor_copy(
-            w2_bf[:].rearrange("p (t m j) -> p m j t", t=PACK, j=PACK),
-            w2_signed[:].rearrange("p j (m t) -> p m j t", t=PACK),
-        )
-        nc.vector.quantize_mx(w2_codes[:].bitcast(FP8X4), w2_plane[:], w2_bf[:])
-        second_product(0, down0, up_relu0)
-        down1 = held.tile([P, PACK, HALF], F32, name="down", tag="down")
-        for t in range(PACK):
-            gather_y(down1, t, n1_sb, 1)
-        second_product(1, down1, up_relu1)
+            for first, count in halves:
+                cols = slice(first, first + count)
+                bank = product(w2_codes, w2_plane, z_codes, z_plane, t, first, count)
+                copy = nc.vector.tensor_copy if t >= 2 and first == 0 else nc.scalar.copy
+                copy(window[t][:, cols], bank)
+                copy(h_plain[t][:, cols], bank)
 
         out_rows = out.rearrange("(p t) j -> p t j", t=PACK)
 
-        def gathered_difference(name, t, lst, halves):
-            diff = held.tile([P, S], F32, name=name)
-            for half in halves:
-                cols = slice(half * HALF, (half + 1) * HALF)
-                nc.vector.tensor_tensor(
-                    diff[:, cols],
-                    h_window[t][:].indirect(entries(lst, half * HALF, HALF)),
-                    h_plain[t][:, cols],
-                    ALU.subtract,
-                )
-            return diff
-
-        def denominator(t):
-            diff = gathered_difference("den%d" % t, t, n4_sb, range(2))
-            size = held.tile([P, S], F32, name="size%d" % t)
-            root = held.tile([P, S], F32, name="root%d" % t)
-            recip = held.tile([P, S], F32, name="recip%d" % t)
-            nc.scalar.activation(size[:], diff[:], ACT.Abs)
-            nc.scalar.activation(root[:], size[:], ACT.Abs_reciprocal_sqrt, bias=0.5)
-            nc.scalar.activation(recip[:], root[:], ACT.Square)
-            return recip
-
-        def quotient(t, recip):
-            diff = gathered_difference("num%d" % t, t, n3_sb, range(2))
-            result = held.tile([P, S], F32, name="result%d" % t)
-            for half in range(2):
-                cols = slice(half * HALF, (half + 1) * HALF)
-                nc.vector.scalar_tensor_tensor(result[:, cols], diff[:, cols], -1.0, recip[:, cols], ALU.mult, ALU.mult)
-                nc.sync.dma_start(out_rows[:, t, cols], result[:, cols])
-
-        recip = denominator(0)
+        den = [held.tile([P, S], F32, name="den%d" % t, tag="diff%d" % t) for t in range(PACK)]
+        size = [held.tile([P, S], F32, name="size%d" % t) for t in range(PACK)]
+        root = [held.tile([P, S], F32, name="root%d" % t) for t in range(PACK)]
+        recip = [held.tile([P, S], F32, name="recip%d" % t) for t in range(PACK)]
         for t in range(PACK):
-            following = denominator(t + 1) if t + 1 < PACK else None
-            quotient(t, recip)
-            recip = following
+            for first, count in halves if t == 0 else whole:
+                gather_difference(den[t], t, n4_sb, h_plain[t], first, count)
+        for step in range(PACK + 2):
+            if step < PACK:
+                nc.scalar.activation(size[step][:], den[step][:], ACT.Abs)
+            if 1 <= step <= PACK:
+                nc.scalar.activation(root[step - 1][:], size[step - 1][:], ACT.Abs_reciprocal_sqrt, bias=0.5)
+            if step >= 2:
+                nc.scalar.activation(recip[step - 2][:], root[step - 2][:], ACT.Square)
+
+        pieces = [(t, 0, S) for t in range(PACK - 1)] + [(PACK - 1, 0, HALF), (PACK - 1, HALF, HALF)]
+        num = [held.tile([P, S], F32, name="num%d" % t, tag="diff%d" % t) for t in range(PACK)]
+        result = [held.tile([P, S], F32, name="result%d" % t) for t in range(PACK)]
+        for step in range(len(pieces) + 1):
+            if step < len(pieces):
+                t, first, count = pieces[step]
+                gather_difference(num[t], t, n3_sb, h_plain[t], first, count)
+            if step >= 1:
+                t, first, count = pieces[step - 1]
+                cols = slice(first, first + count)
+                nc.vector.tensor_tensor(result[t][:, cols], num[t][:, cols], recip[t][:, cols], ALU.mult)
+                nc.sync.dma_start(out_rows[:, t, cols], result[t][:, cols])

@@ -1,6 +1,7 @@
 from contextlib import ExitStack
 
 import concourse.mybir as mybir
+from concourse.masks import make_identity
 
 K, T, S, H, N = 512, 2048, 512, 512, 512
 FLOPS = 2 * K * H * S + 2 * H * N * S
@@ -61,6 +62,9 @@ def tile_picked_hashhingefrac_none_p_kernel(
         window = [held.tile([P, 2 * S], F32, name="window%d" % t) for t in range(PACK)]
         for t in range(PACK):
             nc.gpsimd.memset(window[t][:, S:], 0.0)
+
+        identity = held.tile([P, P], F32, name="identity")
+        make_identity(nc, identity[:])
 
         warm_in = held.tile([P, 1], F32, name="warm_in")
         warm_out = held.tile([P, 1], F32, name="warm_out")
@@ -176,29 +180,41 @@ def tile_picked_hashhingefrac_none_p_kernel(
 
         h_plain = [held.tile([P, S], F32, name="h_plain%d" % t) for t in range(PACK)]
         for t in range(PACK):
-            for first, count in halves:
-                cols = slice(first, first + count)
-                bank = product(w2_codes, w2_plane, z_codes, z_plane, t, first, count)
-                copy = nc.vector.tensor_copy if t >= 2 and first == 0 else nc.scalar.copy
-                copy(window[t][:, cols], bank)
-                copy(h_plain[t][:, cols], bank)
+            for half in range(2):
+                bank = product(w2_codes, w2_plane, z_codes, z_plane, t, half * HALF, HALF)
+                nc.scalar.copy(window[t][:, half_cols(half)], bank)
+            nc.sync.dma_start(h_plain[t][:], window[t][:, :S])
 
         out_rows = out.rearrange("(p t) j -> p t j", t=PACK)
+        blocks = [slice(b * P, (b + 1) * P) for b in range(S // P)]
 
         den = [held.tile([P, S], F32, name="den%d" % t, tag="diff%d" % t) for t in range(PACK)]
         size = [held.tile([P, S], F32, name="size%d" % t) for t in range(PACK)]
         root = [held.tile([P, S], F32, name="root%d" % t) for t in range(PACK)]
-        recip = [held.tile([P, S], F32, name="recip%d" % t) for t in range(PACK)]
+        recip_turned = [held.tile([P, S], F32, name="recip%d" % t) for t in range(PACK)]
+        turned = []
         for t in range(PACK):
-            for first, count in halves if t == 0 else whole:
-                gather_difference(den[t], t, n4_sb, h_plain[t], first, count)
+            nc.vector.tensor_scalar(den[t][:], window[t][:].indirect(n4_sb[:]), -1.0, 0.0, ALU.mult, ALU.add)
+            bank = psum.tile([P, S], F32, name="bank")
+            sources = [(window[t], block) for block in blocks] + [(den[t], block) for block in blocks]
+            for step, (source, block) in enumerate(sources):
+                nc.tensor.matmul(
+                    bank[:, block], source[:, block], identity[:],
+                    start=step == 0, stop=step == len(sources) - 1, is_transpose=True,
+                )
+            turned.append(bank)
+        recip = []
         for step in range(PACK + 2):
             if step < PACK:
-                nc.scalar.activation(size[step][:], den[step][:], ACT.Abs)
+                nc.scalar.activation(size[step][:], turned[step][:], ACT.Abs)
             if 1 <= step <= PACK:
                 nc.scalar.activation(root[step - 1][:], size[step - 1][:], ACT.Abs_reciprocal_sqrt, bias=0.5)
             if step >= 2:
-                nc.scalar.activation(recip[step - 2][:], root[step - 2][:], ACT.Square)
+                nc.scalar.activation(recip_turned[step - 2][:], root[step - 2][:], ACT.Square)
+                bank = psum.tile([P, S], F32, name="bank")
+                for block in blocks:
+                    nc.tensor.transpose(bank[:, block], recip_turned[step - 2][:, block], identity[:])
+                recip.append(bank)
 
         pieces = [(t, 0, S) for t in range(PACK - 1)] + [(PACK - 1, 0, HALF), (PACK - 1, HALF, HALF)]
         num = [held.tile([P, S], F32, name="num%d" % t, tag="diff%d" % t) for t in range(PACK)]

@@ -37,8 +37,12 @@ def tile_picked_hashhingefrac_none_p_kernel(
         held = ctx.enter_context(tc.tile_pool(name="held", bufs=1))
         psum = ctx.enter_context(tc.psum_pool(name="psum", bufs=8))
 
-        offs_sb = held.tile([P, S // 16], U16, name="offs_sb")
-        nc.sync.dma_start(offs_sb[:], offs)
+        def load_lists(name, src):
+            lst = held.tile([P, S // 16], U16, name=name)
+            nc.sync.dma_start(lst[:], src)
+            return lst
+
+        offs_sb = load_lists("offs_sb", offs)
 
         scale_table = held.tile([P, T], U8, name="scale_table", tag="scales_then_w1", align_bytes=64)
         nc.gpsimd.memset(scale_table[:].bitcast(I32), 0)
@@ -48,12 +52,10 @@ def tile_picked_hashhingefrac_none_p_kernel(
 
         gain = held.tile([P, PACK], F32, name="gain")
         nc.sync.dma_start(gain[:], gn.rearrange("(p t) o -> p (t o)", t=PACK))
-        lists = []
-        for name, src in (("n2_sb", n2), ("n1_sb", n1), ("n4_sb", n4), ("n3_sb", n3)):
-            lst = held.tile([P, S // 16], U16, name=name)
-            nc.sync.dma_start(lst[:], src)
-            lists.append(lst)
-        n2_sb, n1_sb, n4_sb, n3_sb = lists
+        n2_sb = load_lists("n2_sb", n2)
+        n1_sb = load_lists("n1_sb", n1)
+        n4_sb = load_lists("n4_sb", n4)
+        n3_sb = load_lists("n3_sb", n3)
         w1_raw = held.tile([P, PACK, H], F32, name="w1_raw")
         nc.sync.dma_start(w1_raw[:], w1.rearrange("(p j) c -> p j c", j=PACK))
         word_table = held.tile([P, T], U32, name="word_table", align_bytes=64)
@@ -61,7 +63,7 @@ def tile_picked_hashhingefrac_none_p_kernel(
 
         window = [held.tile([P, 2 * S], F32, name="window%d" % t) for t in range(PACK)]
         for t in range(PACK):
-            nc.gpsimd.memset(window[t][:, S:], 0.0)
+            nc.vector.memset(window[t][:, S:], 0.0)
 
         identity = held.tile([P, P], F32, name="identity")
         make_identity(nc, identity[:])
@@ -99,6 +101,9 @@ def tile_picked_hashhingefrac_none_p_kernel(
         nc.vector.tensor_scalar(negative[:], gain[:], 0.0, -2.0, ALU.is_lt, ALU.mult)
         nc.vector.tensor_scalar_add(gain_sign[:], negative[:], 1.0)
 
+        gain_neg = held.tile([P, PACK], F32, name="gain_neg")
+        nc.vector.tensor_scalar_mul(gain_neg[:], gain_abs[:], -1.0)
+
         def product(w_codes, w_plane, codes, plane, t, first, count):
             bank = psum.tile([P, S], F32, name="bank")
             rows = slice(t * P, (t + 1) * P)
@@ -125,19 +130,48 @@ def tile_picked_hashhingefrac_none_p_kernel(
         x_codes = held.tile([P, S], U32, name="x_codes", align_bytes=64)
         for first, count in halves:
             nc.vector.tensor_copy(x_codes[:, first : first + count], word_table[:].indirect(entries(offs_sb, first, count)))
-        y_plain = [held.tile([P, S], F32, name="y_plain%d" % t) for t in range(PACK)]
+        y_negated = [held.tile([P, S], F32, name="y_negated%d" % t) for t in range(PACK)]
+        y_banks = []
+        for step in range(PACK + 1):
+            if step < PACK:
+                y_banks.append([])
+                for first, count in halves if step == 0 else whole:
+                    bank = product(w1_codes, w1_plane, x_codes, x_plane, step, first, count)
+                    cols = slice(first, first + count)
+                    nc.scalar.activation(window[step][:, cols], bank, ACT.Copy, scale=gain_abs[:, step : step + 1])
+                    y_banks[step].append((cols, bank))
+            if step >= 1:
+                for cols, bank in y_banks[step - 1]:
+                    nc.scalar.activation(y_negated[step - 1][:, cols], bank, ACT.Copy, scale=gain_neg[:, step - 1 : step])
+
+        blocks = [slice(b * P, (b + 1) * P) for b in range(S // P)]
+
+        def turned_sum(first_term, second_term):
+            bank = psum.tile([P, S], F32, name="bank")
+            sources = [(first_term, block) for block in blocks] + [(second_term, block) for block in blocks]
+            for step, (source, block) in enumerate(sources):
+                nc.tensor.matmul(
+                    bank[:, block], source[:, block], identity[:],
+                    start=step == 0, stop=step == len(sources) - 1, is_transpose=True,
+                )
+            return bank
+
+        up_turned = []
         for t in range(PACK):
-            for first, count in halves if t == 0 else whole:
-                cols = slice(first, first + count)
-                bank = product(w1_codes, w1_plane, x_codes, x_plane, t, first, count)
-                nc.scalar.activation(window[t][:, cols], bank, ACT.Copy, scale=gain_abs[:, t : t + 1])
-                if t < 2:
-                    nc.scalar.activation(y_plain[t][:, cols], bank, ACT.Copy, scale=gain_abs[:, t : t + 1])
-            if t >= 2:
-                nc.sync.dma_start(y_plain[t][:], window[t][:, :S])
+            picked = held.tile([P, S], F32, name="up_picked%d" % t)
+            nc.vector.tensor_copy(picked[:], window[t][:].indirect(n2_sb[:]))
+            up_turned.append(turned_sum(picked, y_negated[t]))
+        up_relu = [psum.tile([P, PACK, P], F32, name="bank") for b in range(len(blocks))]
+        for t in range(PACK):
+            relu_turned = held.tile([P, S], F32, name="relu_turned%d" % t)
+            nc.scalar.activation(relu_turned[:], up_turned[t][:], ACT.Relu, scale=0.5)
+            for b, block in enumerate(blocks):
+                nc.tensor.transpose(up_relu[b][:, t, :], relu_turned[:, block], identity[:])
+        down = held.tile([P, PACK, S], F32, name="down")
+        for t in range(PACK):
+            nc.vector.tensor_tensor(down[:, t, :], window[t][:].indirect(n1_sb[:]), y_negated[t][:], ALU.add)
 
         w2_signed = held.tile([P, PACK, N], BF16, name="w2_signed")
-        w2_bf = held.tile([P, N, PACK], BF16, name="w2_bf", align_bytes=64)
         w2_codes = held.tile([P, N], U32, name="w2_codes", align_bytes=64)
         w2_plane = held.tile([P, N], U8, name="w2_plane", align_bytes=64)
         for j in range(PACK):
@@ -147,47 +181,50 @@ def tile_picked_hashhingefrac_none_p_kernel(
                 ACT.Copy,
                 scale=gain_sign[:, j : j + 1],
             )
-        nc.scalar.copy(
-            w2_bf[:].rearrange("p (c i) j -> p c j i", i=4),
-            w2_signed[:].rearrange("p j (c i) -> p c j i", i=4),
-        )
+        w2_bf = []
+        for t in range(PACK):
+            part = held.tile([P, P, PACK], BF16, name="w2_bf%d" % t, align_bytes=64)
+            nc.scalar.copy(
+                part[:].rearrange("p (c i) j -> p c j i", i=4),
+                w2_signed[:, :, blocks[t]].rearrange("p j (c i) -> p c j i", i=4),
+            )
+            w2_bf.append(part)
 
-        up = held.tile([P, PACK, S], F32, name="up")
-        down = held.tile([P, PACK, S], F32, name="down")
-        for first, count in halves:
-            gather_difference(up[:, 0, :], 0, n2_sb, y_plain[0], first, count)
-            gather_difference(down[:, 0, :], 0, n1_sb, y_plain[0], first, count)
-        gather_difference(up[:, 1, :], 1, n2_sb, y_plain[1], 0, S)
-        gather_difference(down[:, 1, :], 1, n1_sb, y_plain[1], 0, S)
-        for target, lst in ((up, n2_sb), (down, n1_sb)):
-            for t in range(2, PACK):
-                gather_difference(target[:, t, :], t, lst, y_plain[t], 0, S)
-        nc.vector.quantize_mx(w2_codes[:].bitcast(FP8X4), w2_plane[:], w2_bf[:].rearrange("p c j -> p (c j)"))
+        def quantise_w2(t):
+            nc.vector.quantize_mx(
+                w2_codes[:, blocks[t]].bitcast(FP8X4), w2_plane[:, blocks[t]], w2_bf[t][:].rearrange("p c j -> p (c j)")
+            )
 
+        quantise_w2(0)
+        z_bf = held.tile([P, S * PACK], BF16, name="z_bf", align_bytes=64)
         z_codes = held.tile([P, S], U32, name="z_codes", align_bytes=64)
         z_plane = held.tile([P, S], U8, name="z_plane", align_bytes=64)
-        for half in range(2):
-            cols = half_cols(half)
-            up_relu = held.tile([P, HALF, PACK], F32, name="up_relu%d" % half)
-            nc.scalar.activation(up_relu[:], up[:, :, cols].rearrange("p t j -> p j t"), ACT.Relu, scale=0.5)
-            z_bf = held.tile([P, HALF, PACK], BF16, name="z_bf%d" % half, align_bytes=64)
-            nc.vector.scalar_tensor_tensor(
-                z_bf[:], down[:, :, cols].rearrange("p t j -> p j t"), 0.0, up_relu[:], ALU.min, ALU.subtract
-            )
+        z_pieces = ((0, 2 * P), (2 * P, P), (3 * P, P))
+        for first, count in z_pieces:
+            for b in range(first // P, (first + count) // P):
+                nc.vector.scalar_tensor_tensor(
+                    z_bf[:, b * P * PACK : (b + 1) * P * PACK].rearrange("p (j t) -> p j t", t=PACK),
+                    down[:, :, blocks[b]].rearrange("p t j -> p j t"),
+                    0.0,
+                    up_relu[b][:].rearrange("p t j -> p j t"),
+                    ALU.min,
+                    ALU.subtract,
+                )
+            cols = slice(first, first + count)
             nc.vector.quantize_mx(
-                z_codes[:, cols].bitcast(FP8X4), z_plane[:, cols], z_bf[:].rearrange("p j t -> p (j t)")
+                z_codes[:, cols].bitcast(FP8X4), z_plane[:, cols], z_bf[:, first * PACK : (first + count) * PACK]
             )
+        for t in range(1, PACK):
+            quantise_w2(t)
 
         h_plain = [held.tile([P, S], F32, name="h_plain%d" % t) for t in range(PACK)]
         for t in range(PACK):
-            for half in range(2):
-                bank = product(w2_codes, w2_plane, z_codes, z_plane, t, half * HALF, HALF)
-                nc.scalar.copy(window[t][:, half_cols(half)], bank)
+            for first, count in z_pieces if t == 0 else whole:
+                bank = product(w2_codes, w2_plane, z_codes, z_plane, t, first, count)
+                nc.scalar.copy(window[t][:, first : first + count], bank)
             nc.sync.dma_start(h_plain[t][:], window[t][:, :S])
 
         out_rows = out.rearrange("(p t) j -> p t j", t=PACK)
-        blocks = [slice(b * P, (b + 1) * P) for b in range(S // P)]
-
         den = [held.tile([P, S], F32, name="den%d" % t, tag="diff%d" % t) for t in range(PACK)]
         size = [held.tile([P, S], F32, name="size%d" % t) for t in range(PACK)]
         root = [held.tile([P, S], F32, name="root%d" % t) for t in range(PACK)]
@@ -195,14 +232,7 @@ def tile_picked_hashhingefrac_none_p_kernel(
         turned = []
         for t in range(PACK):
             nc.vector.tensor_scalar(den[t][:], window[t][:].indirect(n4_sb[:]), -1.0, 0.0, ALU.mult, ALU.add)
-            bank = psum.tile([P, S], F32, name="bank")
-            sources = [(window[t], block) for block in blocks] + [(den[t], block) for block in blocks]
-            for step, (source, block) in enumerate(sources):
-                nc.tensor.matmul(
-                    bank[:, block], source[:, block], identity[:],
-                    start=step == 0, stop=step == len(sources) - 1, is_transpose=True,
-                )
-            turned.append(bank)
+            turned.append(turned_sum(window[t], den[t]))
         recip = []
         for step in range(PACK + 2):
             if step < PACK:

from contextlib import ExitStack

import concourse.mybir as mybir
from concourse.masks import make_identity

K, T, S, H, N = 512, 2048, 512, 512, 512
FLOPS = 2 * K * H * S + 2 * H * N * S

F32 = mybir.dt.float32
BF16 = mybir.dt.bfloat16
I32 = mybir.dt.int32
U32 = mybir.dt.uint32
U16 = mybir.dt.uint16
U8 = mybir.dt.uint8
FP8X4 = mybir.dt.float8_e4m3fn_x4
ALU = mybir.AluOpType
ACT = mybir.ActivationFunctionType

P = 128
PACK = 4
HALF = S // 2


def entries(lists, first, count):
    return lists[:, first // 16 : (first + count) // 16]


def half_cols(half):
    return slice(half * HALF, (half + 1) * HALF)


def tile_picked_hashhingefrac_none_p_kernel(
    tc, x_words, x_scales, w1, gn, w2, offs, n1, n2, n3, n4, out
):
    nc = tc.nc
    with ExitStack() as ctx:
        held = ctx.enter_context(tc.tile_pool(name="held", bufs=1))
        psum = ctx.enter_context(tc.psum_pool(name="psum", bufs=8))

        def load_lists(name, src):
            lst = held.tile([P, S // 16], U16, name=name)
            nc.sync.dma_start(lst[:], src)
            return lst

        offs_sb = load_lists("offs_sb", offs)

        scale_table = held.tile([P, T], U8, name="scale_table", tag="scales_then_w1", align_bytes=64)
        nc.gpsimd.memset(scale_table[:].bitcast(I32), 0)
        nc.scalar.dma_start(scale_table[0:P:8, :].bitcast(I32), x_scales[0].bitcast(I32))
        x_plane = held.tile([P, S], U8, name="x_plane", align_bytes=64)
        nc.gpsimd.memset(x_plane[:].bitcast(I32), 0)

        gain = held.tile([P, PACK], F32, name="gain")
        nc.sync.dma_start(gain[:], gn.rearrange("(p t) o -> p (t o)", t=PACK))
        n2_sb = load_lists("n2_sb", n2)
        n1_sb = load_lists("n1_sb", n1)
        n4_sb = load_lists("n4_sb", n4)
        n3_sb = load_lists("n3_sb", n3)
        w1_raw = held.tile([P, PACK, H], F32, name="w1_raw")
        nc.sync.dma_start(w1_raw[:], w1.rearrange("(p j) c -> p j c", j=PACK))
        word_table = held.tile([P, T], U32, name="word_table", align_bytes=64)
        nc.sync.dma_start(word_table[:].bitcast(I32), x_words[0].rearrange("p n t -> p (n t)").bitcast(I32))

        window = [held.tile([P, 2 * S], F32, name="window%d" % t) for t in range(PACK)]
        for t in range(PACK):
            nc.vector.memset(window[t][:, S:], 0.0)

        identity = held.tile([P, P], F32, name="identity")
        make_identity(nc, identity[:])

        warm_in = held.tile([P, 1], F32, name="warm_in")
        warm_out = held.tile([P, 1], F32, name="warm_out")
        nc.vector.memset(warm_in[:], 1.0)
        nc.scalar.activation(warm_out[:], warm_in[:], ACT.Abs_reciprocal_sqrt)

        picked_scales = held.tile([P, S], U8, name="picked_scales", tag="picked_then_w2", align_bytes=64)
        nc.vector.tensor_copy(picked_scales[:], scale_table[:].indirect(offs_sb[:]))
        for q in range(4):
            nc.scalar.dma_start(
                x_plane[32 * q : 32 * q + 4, :].bitcast(I32),
                picked_scales[32 * q : 32 * q + 32 : 8, :].bitcast(I32),
            )
        w2_raw = held.tile([P, PACK, N], F32, name="w2_raw", tag="picked_then_w2", align_bytes=64)
        nc.sync.dma_start(w2_raw[:], w2.rearrange("(p j) c -> p j c", j=PACK))

        w1_codes = held.tile([P, H], U32, name="w1_codes", align_bytes=64)
        w1_plane = held.tile([P, H], U8, name="w1_plane", align_bytes=64)
        w1_dealt = w1_raw[:].rearrange("p j (m t) -> p m j t", t=PACK)
        w1_low = held.tile([P, 2 * H], BF16, name="w1_low", tag="scales_then_w1", align_bytes=64)
        w1_high = held.tile([P, 2 * H], BF16, name="w1_high", align_bytes=64)
        nc.vector.tensor_copy(w1_low[:].rearrange("p (t m j) -> p m j t", t=2, j=PACK), w1_dealt[:, :, :, 0:2])
        nc.scalar.copy(w1_high[:].rearrange("p (t m j) -> p m j t", t=2, j=PACK), w1_dealt[:, :, :, 2:4])
        for pair, w1_bf in enumerate((w1_low, w1_high)):
            cols = slice(pair * 2 * P, (pair + 1) * 2 * P)
            nc.vector.quantize_mx(w1_codes[:, cols].bitcast(FP8X4), w1_plane[:, cols], w1_bf[:])

        gain_abs = held.tile([P, PACK], F32, name="gain_abs")
        nc.scalar.activation(gain_abs[:], gain[:], ACT.Abs)
        negative = held.tile([P, PACK], F32, name="negative")
        gain_sign = held.tile([P, PACK], F32, name="gain_sign")
        nc.vector.tensor_scalar(negative[:], gain[:], 0.0, -2.0, ALU.is_lt, ALU.mult)
        nc.vector.tensor_scalar_add(gain_sign[:], negative[:], 1.0)

        gain_neg = held.tile([P, PACK], F32, name="gain_neg")
        nc.vector.tensor_scalar_mul(gain_neg[:], gain_abs[:], -1.0)

        def product(w_codes, w_plane, codes, plane, t, first, count):
            bank = psum.tile([P, S], F32, name="bank")
            rows = slice(t * P, (t + 1) * P)
            cols = slice(first, first + count)
            nc.tensor.matmul_mx(
                bank[:, :count],
                lhsT=w_codes[:, rows].bitcast(FP8X4),
                lhsT_scale=w_plane[:, rows],
                rhs=codes[:, cols].bitcast(FP8X4),
                rhs_scale=plane[:, cols],
                start=True,
                stop=True,
            )
            return bank[:, :count]

        def gather_difference(target, t, lst, plain, first, count):
            cols = slice(first, first + count)
            nc.vector.tensor_tensor(
                target[:, cols], window[t][:].indirect(entries(lst, first, count)), plain[:, cols], ALU.subtract
            )

        halves = ((0, HALF), (HALF, HALF))
        whole = ((0, S),)
        x_codes = held.tile([P, S], U32, name="x_codes", align_bytes=64)
        for first, count in halves:
            nc.vector.tensor_copy(x_codes[:, first : first + count], word_table[:].indirect(entries(offs_sb, first, count)))
        y_negated = [held.tile([P, S], F32, name="y_negated%d" % t) for t in range(PACK)]
        y_banks = []
        for step in range(PACK + 1):
            if step < PACK:
                y_banks.append([])
                for first, count in halves if step == 0 else whole:
                    bank = product(w1_codes, w1_plane, x_codes, x_plane, step, first, count)
                    cols = slice(first, first + count)
                    nc.scalar.activation(window[step][:, cols], bank, ACT.Copy, scale=gain_abs[:, step : step + 1])
                    y_banks[step].append((cols, bank))
            if step >= 1:
                for cols, bank in y_banks[step - 1]:
                    nc.scalar.activation(y_negated[step - 1][:, cols], bank, ACT.Copy, scale=gain_neg[:, step - 1 : step])

        blocks = [slice(b * P, (b + 1) * P) for b in range(S // P)]

        def turned_sum(first_term, second_term):
            bank = psum.tile([P, S], F32, name="bank")
            sources = [(first_term, block) for block in blocks] + [(second_term, block) for block in blocks]
            for step, (source, block) in enumerate(sources):
                nc.tensor.matmul(
                    bank[:, block], source[:, block], identity[:],
                    start=step == 0, stop=step == len(sources) - 1, is_transpose=True,
                )
            return bank

        up_turned = []
        for t in range(PACK):
            picked = held.tile([P, S], F32, name="up_picked%d" % t)
            nc.vector.tensor_copy(picked[:], window[t][:].indirect(n2_sb[:]))
            up_turned.append(turned_sum(picked, y_negated[t]))
        up_relu = [psum.tile([P, PACK, P], F32, name="bank") for b in range(len(blocks))]
        for t in range(PACK):
            relu_turned = held.tile([P, S], F32, name="relu_turned%d" % t)
            nc.scalar.activation(relu_turned[:], up_turned[t][:], ACT.Relu, scale=0.5)
            for b, block in enumerate(blocks):
                nc.tensor.transpose(up_relu[b][:, t, :], relu_turned[:, block], identity[:])
        down = held.tile([P, PACK, S], F32, name="down")
        for t in range(PACK):
            nc.vector.tensor_tensor(down[:, t, :], window[t][:].indirect(n1_sb[:]), y_negated[t][:], ALU.add)

        w2_signed = held.tile([P, PACK, N], BF16, name="w2_signed")
        w2_codes = held.tile([P, N], U32, name="w2_codes", align_bytes=64)
        w2_plane = held.tile([P, N], U8, name="w2_plane", align_bytes=64)
        for j in range(PACK):
            nc.scalar.activation(
                w2_signed[:, j, :].rearrange("p (t m) -> p m t", t=PACK),
                w2_raw[:, j, :].rearrange("p (m t) -> p m t", t=PACK),
                ACT.Copy,
                scale=gain_sign[:, j : j + 1],
            )
        w2_bf = []
        for t in range(PACK):
            part = held.tile([P, P, PACK], BF16, name="w2_bf%d" % t, align_bytes=64)
            nc.scalar.copy(
                part[:].rearrange("p (c i) j -> p c j i", i=4),
                w2_signed[:, :, blocks[t]].rearrange("p j (c i) -> p c j i", i=4),
            )
            w2_bf.append(part)

        def quantise_w2(t):
            nc.vector.quantize_mx(
                w2_codes[:, blocks[t]].bitcast(FP8X4), w2_plane[:, blocks[t]], w2_bf[t][:].rearrange("p c j -> p (c j)")
            )

        quantise_w2(0)
        z_bf = held.tile([P, S * PACK], BF16, name="z_bf", align_bytes=64)
        z_codes = held.tile([P, S], U32, name="z_codes", align_bytes=64)
        z_plane = held.tile([P, S], U8, name="z_plane", align_bytes=64)
        z_pieces = ((0, 2 * P), (2 * P, P), (3 * P, P))
        for first, count in z_pieces:
            for b in range(first // P, (first + count) // P):
                nc.vector.scalar_tensor_tensor(
                    z_bf[:, b * P * PACK : (b + 1) * P * PACK].rearrange("p (j t) -> p j t", t=PACK),
                    down[:, :, blocks[b]].rearrange("p t j -> p j t"),
                    0.0,
                    up_relu[b][:].rearrange("p t j -> p j t"),
                    ALU.min,
                    ALU.subtract,
                )
            cols = slice(first, first + count)
            nc.vector.quantize_mx(
                z_codes[:, cols].bitcast(FP8X4), z_plane[:, cols], z_bf[:, first * PACK : (first + count) * PACK]
            )
        for t in range(1, PACK):
            quantise_w2(t)

        h_plain = [held.tile([P, S], F32, name="h_plain%d" % t) for t in range(PACK)]
        for t in range(PACK):
            for first, count in z_pieces if t == 0 else whole:
                bank = product(w2_codes, w2_plane, z_codes, z_plane, t, first, count)
                nc.scalar.copy(window[t][:, first : first + count], bank)
            nc.sync.dma_start(h_plain[t][:], window[t][:, :S])

        out_rows = out.rearrange("(p t) j -> p t j", t=PACK)
        den = [held.tile([P, S], F32, name="den%d" % t, tag="diff%d" % t) for t in range(PACK)]
        size = [held.tile([P, S], F32, name="size%d" % t) for t in range(PACK)]
        root = [held.tile([P, S], F32, name="root%d" % t) for t in range(PACK)]
        recip_turned = [held.tile([P, S], F32, name="recip%d" % t) for t in range(PACK)]
        turned = []
        for t in range(PACK):
            nc.vector.tensor_scalar(den[t][:], window[t][:].indirect(n4_sb[:]), -1.0, 0.0, ALU.mult, ALU.add)
            turned.append(turned_sum(window[t], den[t]))
        recip = []
        for step in range(PACK + 2):
            if step < PACK:
                nc.scalar.activation(size[step][:], turned[step][:], ACT.Abs)
            if 1 <= step <= PACK:
                nc.scalar.activation(root[step - 1][:], size[step - 1][:], ACT.Abs_reciprocal_sqrt, bias=0.5)
            if step >= 2:
                nc.scalar.activation(recip_turned[step - 2][:], root[step - 2][:], ACT.Square)
                bank = psum.tile([P, S], F32, name="bank")
                for block in blocks:
                    nc.tensor.transpose(bank[:, block], recip_turned[step - 2][:, block], identity[:])
                recip.append(bank)

        pieces = [(t, 0, S) for t in range(PACK - 1)] + [(PACK - 1, 0, HALF), (PACK - 1, HALF, HALF)]
        num = [held.tile([P, S], F32, name="num%d" % t, tag="diff%d" % t) for t in range(PACK)]
        result = [held.tile([P, S], F32, name="result%d" % t) for t in range(PACK)]
        for step in range(len(pieces) + 1):
            if step < len(pieces):
                t, first, count = pieces[step]
                gather_difference(num[t], t, n3_sb, h_plain[t], first, count)
            if step >= 1:
                t, first, count = pieces[step - 1]
                cols = slice(first, first + count)
                nc.vector.tensor_tensor(result[t][:, cols], num[t][:, cols], recip[t][:, cols], ALU.mult)
                nc.sync.dma_start(out_rows[:, t, cols], result[t][:, cols])
